import numpy as np
import ml_dtypes


def mxq(x, axis, fmt="e4m3"):
    dtype, down = {"e4m3": (ml_dtypes.float8_e4m3fn, 7), "e5m2": (ml_dtypes.float8_e5m2, 14)}[fmt]
    v = np.moveaxis(np.asarray(x, np.float32).astype(ml_dtypes.bfloat16).astype(np.float64), axis, -1)
    blocks = v.reshape(v.shape[:-1] + (-1, 32))
    amax = np.abs(blocks).max(-1, keepdims=True)
    byte = np.maximum(np.where(amax > 0, np.frexp(amax)[1] - 1 + 127, 0) - down, 1)
    scale = np.exp2(byte - 127.0)
    codes = (blocks / scale).astype(np.float32).astype(dtype).astype(np.float64)
    return np.moveaxis((codes * scale).reshape(v.shape), -1, axis)


WIDE = False


def mx_kscale(k):
    if not WIDE:
        return np.ones(k)
    levels = np.array([10, -10, 5, -5, 0])
    if k % 512:
        return np.exp2(np.random.permutation(np.resize(levels, k // 32))).repeat(32)
    a = np.empty((k // 512, 16))
    for p in range(k // 512):
        a[p, :8] = np.random.permutation(np.resize(levels, 8))
        for g in range(8):
            far = levels[np.abs(levels - a[p, g]) >= 10]
            a[p, g + 8] = far[np.random.randint(len(far))]
    return np.exp2(a.ravel()).repeat(32)


def f64(x):
    return np.asarray(x).astype(np.float64)


def striped(idx):
    return np.tile(idx.reshape(-1, 16).T, (8, 1)).astype(np.uint16)


def unstriped(offs):
    return offs[:16].T.reshape(-1).astype(np.int64)


def striped8(idx):
    return np.concatenate([x.reshape(-1, 16).T for x in idx]).astype(np.uint16)


def runs(offs, k):
    lists = np.stack([offs[16 * r : 16 * r + 16].T.reshape(-1) for r in range(8)]).astype(np.int64)
    return lists[np.arange(k) % 512 // 64]


def pack_weight(w):
    k, n = w.shape
    w = f64(np.asarray(w, np.float32).astype(ml_dtypes.bfloat16)).reshape(k // 32, 32, n)
    amax = np.abs(w).max(1)
    byte = np.clip(np.where(amax > 0, np.frexp(amax)[1] - 1 + 127 - 7, 1), 1, 254)
    scaled = (w * np.exp2(127.0 - byte)[:, None, :]).reshape(k, n).astype(np.float32)
    words = np.ascontiguousarray(scaled.reshape(k // 512, 128, 4, n).transpose(0, 1, 3, 2)).astype(ml_dtypes.float8_e4m3fn).view(np.uint8)
    return words, np.ascontiguousarray(byte.astype(np.uint8).reshape(k // 512, 16, n))


def unpack_weight(words, scales):
    g, p, n, _ = words.shape
    vals = np.ascontiguousarray(words).view(ml_dtypes.float8_e4m3fn).astype(np.float64) * np.repeat(np.exp2(scales.astype(np.float64) - 127.0), 8, axis=1)[..., None]
    return vals.transpose(0, 1, 3, 2).reshape(g * 512, n)


def relu(v):
    return np.maximum(v, 0.0)


def sigmoid(v):
    return 1.0 / (1.0 + np.exp(-np.maximum(v, -700.0)))


K, T, S, V, N, H = 512, 2048, 512, 256, 512, 512


def setup_inputs():
    n = np.random.standard_normal
    s = mx_kscale(K)[:, None]
    u = mx_kscale(H)
    packed_xT = pack_weight(n((K, T)) * s)
    return {
        "x_words": packed_xT[0],
        "x_scales": packed_xT[1],
        "w1": (n((K, H)) / np.sqrt(K) / s).astype(np.float32),
        "w2": (n((K, H)) / np.sqrt(K) / s).astype(np.float32),
        "gn": (np.random.uniform(0.5, 1.5, (H, 1)) * u[:, None]).astype(np.float32),
        "w3": (n((H, N)) / np.sqrt(H) / u[:, None]).astype(np.float32),
        "res": (2 * n((N, V))).astype(np.float32),
        "offs": striped(np.random.permutation(T)[:S]),
        "two": striped(np.random.permutation(T)[:S]),
        "ba": striped8(np.stack([np.random.permutation(S)[:V] for _ in range(8)])),
        "bb": striped8(np.stack([np.random.permutation(S)[:V] for _ in range(8)])),
    }


def reference(x_words, x_scales, w1, w2, gn, w3, res, offs, two, ba, bb):
    xq = unpack_weight(x_words, x_scales)[:, unstriped(offs)]
    y = mxq(f64(w1), 0, "e4m3").T @ xq
    x_two = unpack_weight(x_words, x_scales)[:, unstriped(two)]
    c = sigmoid(mxq(f64(w2), 0, "e4m3").T @ x_two)
    hi = y + c
    lo = y - c
    sh = relu(np.minimum(hi[np.arange(H)[:, None], runs(ba, H)], hi[np.arange(H)[:, None], runs(bb, H)]) - (np.maximum(lo[np.arange(H)[:, None], runs(ba, H)], lo[np.arange(H)[:, None], runs(bb, H)])))
    un = np.maximum(hi[np.arange(H)[:, None], runs(ba, H)], hi[np.arange(H)[:, None], runs(bb, H)]) - (np.minimum(lo[np.arange(H)[:, None], runs(ba, H)], lo[np.arange(H)[:, None], runs(bb, H)]))
    z = f64(gn) * (sh / (un + 0.1))
    return f64(res) + (mxq(f64(w3), 0, "e4m3").T @ mxq(z, 0, "e4m3"))

@@ -1,0 +1,159 @@
+from contextlib import ExitStack
+
+import concourse.mybir as mybir
+
+K, T, S, V, N, H = 512, 2048, 512, 256, 512, 512
+P = 128
+PACK = 4
+FLOPS = 2 * K * H * S * 2 + 2 * H * N * V
+
+F32 = mybir.dt.float32
+BF16 = mybir.dt.bfloat16
+I32 = mybir.dt.int32
+U32 = mybir.dt.uint32
+U16 = mybir.dt.uint16
+U8 = mybir.dt.uint8
+FP8X4 = mybir.dt.float8_e4m3fn_x4
+ALU = mybir.AluOpType
+ACT = mybir.ActivationFunctionType
+
+
+def tile_picked_boxiou_none_p_kernel(tc, x_words, x_scales, w1, w2, gn, w3, res, offs, two, ba, bb, out):
+    nc = tc.nc
+    with ExitStack() as ctx:
+        keep = ctx.enter_context(tc.tile_pool(name="keep", bufs=1))
+        psum = ctx.enter_context(tc.psum_pool(name="psum", bufs=1))
+
+        def sb(name, shape, dtype):
+            return keep.tile(shape, dtype, name=name, align_bytes=64)
+
+        offs_t = sb("offs_t", [P, S // 16], U16)
+        two_t = sb("two_t", [P, S // 16], U16)
+        ba_t = sb("ba_t", [P, V // 16], U16)
+        bb_t = sb("bb_t", [P, V // 16], U16)
+        xw = sb("xw", [P, T], U32)
+        xs = sb("xs", [P, T], U8)
+        w1_raw = sb("w1_raw", [P, PACK, H], F32)
+        w2_raw = sb("w2_raw", [P, PACK, H], F32)
+        w3_raw = sb("w3_raw", [P, PACK, N], F32)
+        res_t = sb("res_t", [P, N // P, V], F32)
+        gn_t = [sb(f"gn{t}", [P, 1], F32) for t in range(PACK)]
+        warm = sb("warm", [P, 2], F32)
+
+        nc.vector.memset(xs[:].bitcast(I32), 0)
+        nc.vector.memset(warm[:, 0:1], 0.0)
+
+        nc.sync.dma_start(offs_t[:], offs)
+        nc.sync.dma_start(w1_raw[:], w1.rearrange("(p j) c -> p j c", j=PACK))
+        for q in range(4):
+            nc.scalar.dma_start(xs[32 * q : 32 * q + 4, :].bitcast(I32), x_scales[0, 4 * q : 4 * q + 4, :].bitcast(I32))
+        nc.scalar.activation(warm[:, 1:2], warm[:, 0:1], ACT.Sigmoid)
+        nc.sync.dma_start(two_t[:], two)
+        nc.sync.dma_start(xw[:].bitcast(I32), x_words[0].rearrange("p c r -> p (c r)").bitcast(I32))
+        nc.sync.dma_start(w2_raw[:], w2.rearrange("(p j) c -> p j c", j=PACK))
+        nc.sync.dma_start(ba_t[:], ba)
+        nc.sync.dma_start(bb_t[:], bb)
+        w3_rows = w3.rearrange("(b j r) n -> j b r n", j=PACK, r=8)
+        for j in range(PACK):
+            nc.sync.dma_start(w3_raw[:, j, :], w3_rows[j])
+        nc.sync.dma_start(res_t[:], res.rearrange("(t p) v -> p t v", p=P))
+        gn_rows = gn.rearrange("(b j r) o -> j b r o", j=PACK, r=8)
+        with nc.allow_non_contiguous_dma(reason="one gain for each feature"):
+            for t in range(PACK):
+                nc.sync.dma_start(gn_t[t][:], gn_rows[t])
+
+        xa_s = sb("xa_s", [P, S], U8)
+        xb_s = sb("xb_s", [P, S], U8)
+        xa_w = sb("xa_w", [P, S], U32)
+        xb_w = sb("xb_w", [P, S], U32)
+        nc.vector.tensor_copy(xa_s[:], xs[:].indirect(offs_t[:]))
+        nc.vector.tensor_copy(xb_s[:], xs[:].indirect(two_t[:]))
+
+        def cast_tile(copy, name, raw, t):
+            g = sb(f"{name}_g{t}", [P, P * PACK], BF16)
+            src = raw[:].rearrange("p j (b t r) -> p t b r j", t=PACK, r=8)[:, t]
+            copy(g[:].rearrange("p (b r j) -> p b r j", r=8, j=PACK), src)
+            return g
+
+        def quant(name, g, cols):
+            codes = sb(f"{name}_c", [P, cols], U32)
+            scales = sb(f"{name}_s", [P, cols], U8)
+            nc.vector.quantize_mx(out=codes[:].bitcast(FP8X4), scales=scales[:], in_=g)
+            return codes, scales
+
+        def product(bank, wq, xw_g, xs_g):
+            nc.tensor.matmul_mx(out=bank, lhsT=wq[0].bitcast(FP8X4), lhsT_scale=wq[1], rhs=xw_g.bitcast(FP8X4), rhs_scale=xs_g, start=True, stop=True)
+
+        w1_g = [cast_tile(nc.scalar.copy, "w1", w1_raw, t) for t in range(PACK)]
+        w1_q = [quant(f"w1q{t}", w1_g[t][:], P) for t in range(PACK)]
+        nc.vector.tensor_copy(xa_w[:], xw[:].indirect(offs_t[:]))
+        nc.vector.tensor_copy(xb_w[:], xw[:].indirect(two_t[:]))
+
+        y_sb = []
+        for t in range(PACK):
+            bank = psum.tile([P, S], F32, name=f"ybank{t}", tag=f"ybank{t}")
+            product(bank[:], (w1_q[t][0][:], w1_q[t][1][:]), xa_w[:], xa_s[:])
+            y = sb(f"y{t}", [P, S], F32)
+            nc.scalar.copy(y[:], bank[:])
+            y_sb.append(y)
+
+        w2_g = [cast_tile(nc.vector.tensor_copy if t < 2 else nc.scalar.copy, "w2", w2_raw, t) for t in range(PACK)]
+        w2_q = [quant(f"w2q{t}", w2_g[t][:], P) for t in range(PACK)]
+
+        ya = sb("ya", [P, PACK, V], F32)
+        dy = sb("dy", [P, PACK, V], F32)
+        ca = sb("ca", [P, PACK, V], F32)
+        cb = sb("cb", [P, PACK, V], F32)
+        ad = sb("ad", [P, PACK, V], F32)
+        for h in range(2):
+            for t in (2 * h, 2 * h + 1):
+                nc.vector.tensor_copy(ya[:, t, :], y_sb[t][:].indirect(ba_t[:]))
+            for t in (2 * h, 2 * h + 1):
+                nc.vector.tensor_tensor(dy[:, t, :], y_sb[t][:].indirect(bb_t[:]), ya[:, t, :], ALU.subtract)
+        for t in range(PACK):
+            bank = psum.tile([P, S], F32, name=f"ubank{t}", tag=f"ubank{t}")
+            product(bank[:], (w2_q[t][0][:], w2_q[t][1][:]), xb_w[:], xb_s[:])
+            u = sb(f"u{t}", [P, S], F32)
+            nc.scalar.copy(u[:], bank[:])
+            nc.scalar.activation(ca[:, t, :], u[:].indirect(ba_t[:]), ACT.Sigmoid)
+            nc.scalar.activation(cb[:, t, :], u[:].indirect(bb_t[:]), ACT.Sigmoid)
+            if t % 2:
+                nc.scalar.activation(ad[:, t - 1 : t + 1, :], dy[:, t - 1 : t + 1, :], ACT.Abs)
+
+        sm = sb("sm", [P, PACK, V], F32)
+        mx = sb("mx", [P, PACK, V], F32)
+        wide = sb("wide", [P, PACK, V], F32)
+        num = sb("num", [P, PACK, V], F32)
+        un = sb("un", [P, PACK, V], F32)
+        rs = sb("rs", [P, PACK, V], F32)
+        q1 = sb("q1", [P, PACK, V], F32)
+        z = sb("z", [P, PACK, V], BF16)
+        halves = [slice(0, 2), slice(2, 4)]
+        for h in halves:
+            nc.vector.tensor_tensor(sm[:, h, :], ca[:, h, :], cb[:, h, :], ALU.add)
+            nc.vector.tensor_tensor(mx[:, h, :], ca[:, h, :], cb[:, h, :], ALU.max)
+            nc.vector.tensor_tensor(wide[:, h, :], sm[:, h, :], ad[:, h, :], ALU.add)
+            nc.vector.scalar_tensor_tensor(un[:, h, :], mx[:, h, :], 2.0, wide[:, h, :], ALU.mult, ALU.max)
+            nc.vector.scalar_tensor_tensor(num[:, h, :], sm[:, h, :], 2.0, un[:, h, :], ALU.mult, ALU.subtract)
+        for h in halves:
+            nc.scalar.activation(rs[:, h, :], un[:, h, :], ACT.Abs_reciprocal_sqrt, bias=0.1)
+
+        w3_g = sb("w3_g", [P, N, PACK], BF16)
+        nc.scalar.copy(w3_g[:], w3_raw[:].rearrange("p j n -> p n j"))
+        w3_q = quant("w3q", w3_g[:].rearrange("p n j -> p (n j)"), N)
+
+        for h in halves:
+            nc.vector.scalar_tensor_tensor(q1[:, h, :], num[:, h, :], 0.0, rs[:, h, :], ALU.max, ALU.mult)
+        for t in range(PACK):
+            nc.vector.scalar_tensor_tensor(z[:, t, :], q1[:, t, :], gn_t[t][:], rs[:, t, :], ALU.mult, ALU.mult)
+        z_g = sb("z_g", [P, V, PACK], BF16)
+        nc.vector.tensor_copy(z_g[:], z[:].rearrange("p t v -> p v t"))
+        z_q = quant("zq", z_g[:].rearrange("p v t -> p (v t)"), V)
+
+        for m in range(N // P):
+            bank = psum.tile([P, S], F32, name=f"obank{m}", tag=f"ybank{m}")
+            cols = slice(m * P, (m + 1) * P)
+            product(bank[:, :V], (w3_q[0][:, cols], w3_q[1][:, cols]), z_q[0][:], z_q[1][:])
+            o = sb(f"o{m}", [P, V], F32)
+            nc.vector.tensor_tensor(o[:], bank[:, :V], res_t[:, m, :], ALU.add)
+            nc.sync.dma_start(out[cols, :], o[:])

@@ -24,8 +24,8 @@ def tile_picked_boxiou_none_p_kernel(tc, x_words, x_scales, w1, w2, gn, w3, res,
         keep = ctx.enter_context(tc.tile_pool(name="keep", bufs=1))
         psum = ctx.enter_context(tc.psum_pool(name="psum", bufs=1))
 
-        def sb(name, shape, dtype):
-            return keep.tile(shape, dtype, name=name, align_bytes=64)
+        def sb(name, shape, dtype, tag=None):
+            return keep.tile(shape, dtype, name=name, tag=tag or name, align_bytes=64)
 
         offs_t = sb("offs_t", [P, S // 16], U16)
         two_t = sb("two_t", [P, S // 16], U16)
@@ -64,15 +64,13 @@ def tile_picked_boxiou_none_p_kernel(tc, x_words, x_scales, w1, w2, gn, w3, res,
 
         xa_s = sb("xa_s", [P, S], U8)
         xb_s = sb("xb_s", [P, S], U8)
-        xa_w = sb("xa_w", [P, S], U32)
-        xb_w = sb("xb_w", [P, S], U32)
         nc.vector.tensor_copy(xa_s[:], xs[:].indirect(offs_t[:]))
         nc.vector.tensor_copy(xb_s[:], xs[:].indirect(two_t[:]))
 
-        def cast_tile(copy, name, raw, t):
-            g = sb(f"{name}_g{t}", [P, P * PACK], BF16)
-            src = raw[:].rearrange("p j (b t r) -> p t b r j", t=PACK, r=8)[:, t]
-            copy(g[:].rearrange("p (b r j) -> p b r j", r=8, j=PACK), src)
+        def cast_tile(copy, name, raw, t, tag=None):
+            g = sb(name, [P, P * PACK], BF16, tag)
+            src = raw[:].rearrange("p j (b t h i) -> p t b h j i", t=PACK, h=2, i=4)[:, t]
+            copy(g[:].rearrange("p (b h i j) -> p b h j i", h=2, i=4, j=PACK), src)
             return g
 
         def quant(name, g, cols):
@@ -84,32 +82,41 @@ def tile_picked_boxiou_none_p_kernel(tc, x_words, x_scales, w1, w2, gn, w3, res,
         def product(bank, wq, xw_g, xs_g):
             nc.tensor.matmul_mx(out=bank, lhsT=wq[0].bitcast(FP8X4), lhsT_scale=wq[1], rhs=xw_g.bitcast(FP8X4), rhs_scale=xs_g, start=True, stop=True)
 
-        w1_g = [cast_tile(nc.scalar.copy, "w1", w1_raw, t) for t in range(PACK)]
+        w1_g = [cast_tile(nc.scalar.copy, f"w1g{t}", w1_raw, t) for t in range(PACK)]
         w1_q = [quant(f"w1q{t}", w1_g[t][:], P) for t in range(PACK)]
+        xa_w = sb("xa_w", [P, S], U32, "w1g2")
+        xb_w = sb("xb_w", [P, S], U32)
         nc.vector.tensor_copy(xa_w[:], xw[:].indirect(offs_t[:]))
         nc.vector.tensor_copy(xb_w[:], xw[:].indirect(two_t[:]))
 
-        y_sb = []
-        for t in range(PACK):
+        def middles(t):
             bank = psum.tile([P, S], F32, name=f"ybank{t}", tag=f"ybank{t}")
             product(bank[:], (w1_q[t][0][:], w1_q[t][1][:]), xa_w[:], xa_s[:])
             y = sb(f"y{t}", [P, S], F32)
             nc.scalar.copy(y[:], bank[:])
-            y_sb.append(y)
+            return y
 
-        w2_g = [cast_tile(nc.vector.tensor_copy if t < 2 else nc.scalar.copy, "w2", w2_raw, t) for t in range(PACK)]
-        w2_q = [quant(f"w2q{t}", w2_g[t][:], P) for t in range(PACK)]
-
-        ya = sb("ya", [P, PACK, V], F32)
         dy = sb("dy", [P, PACK, V], F32)
+
+        def gaps(h, tag):
+            ya = sb(f"ya{h}", [P, 2, V], F32, tag)
+            for e in range(2):
+                nc.vector.tensor_copy(ya[:, e, :], y_sb[2 * h + e][:].indirect(ba_t[:]))
+            for e in range(2):
+                nc.vector.tensor_tensor(dy[:, 2 * h + e, :], y_sb[2 * h + e][:].indirect(bb_t[:]), ya[:, e, :], ALU.subtract)
+
+        y_sb = [middles(0), middles(1)]
+        w2_g = [cast_tile(nc.vector.tensor_copy, f"w2g{t}", w2_raw, t, f"w1g{t}") for t in range(2)]
+        w2_q = [quant(f"w2q{t}", w2_g[t][:], P) for t in range(2)]
+        w2_g += [cast_tile(nc.scalar.copy, f"w2g{t}", w2_raw, t, f"w1q{t - 2}_c") for t in range(2, PACK)]
+        y_sb += [middles(2), middles(3)]
+        gaps(0, "w1g0")
+        w2_q += [quant(f"w2q{t}", w2_g[t][:], P) for t in range(2, PACK)]
+        gaps(1, "w1q1_c")
+
         ca = sb("ca", [P, PACK, V], F32)
         cb = sb("cb", [P, PACK, V], F32)
         ad = sb("ad", [P, PACK, V], F32)
-        for h in range(2):
-            for t in (2 * h, 2 * h + 1):
-                nc.vector.tensor_copy(ya[:, t, :], y_sb[t][:].indirect(ba_t[:]))
-            for t in (2 * h, 2 * h + 1):
-                nc.vector.tensor_tensor(dy[:, t, :], y_sb[t][:].indirect(bb_t[:]), ya[:, t, :], ALU.subtract)
         for t in range(PACK):
             bank = psum.tile([P, S], F32, name=f"ubank{t}", tag=f"ubank{t}")
             product(bank[:], (w2_q[t][0][:], w2_q[t][1][:]), xb_w[:], xb_s[:])
@@ -125,9 +132,9 @@ def tile_picked_boxiou_none_p_kernel(tc, x_words, x_scales, w1, w2, gn, w3, res,
         wide = sb("wide", [P, PACK, V], F32)
         num = sb("num", [P, PACK, V], F32)
         un = sb("un", [P, PACK, V], F32)
-        rs = sb("rs", [P, PACK, V], F32)
-        q1 = sb("q1", [P, PACK, V], F32)
-        z = sb("z", [P, PACK, V], BF16)
+        rs = sb("rs", [P, PACK, V], F32, "u3")
+        rec = sb("rec", [P, PACK, V], F32)
+        gained = sb("gained", [P, PACK, V], F32)
         halves = [slice(0, 2), slice(2, 4)]
         for h in halves:
             nc.vector.tensor_tensor(sm[:, h, :], ca[:, h, :], cb[:, h, :], ALU.add)
@@ -135,25 +142,35 @@ def tile_picked_boxiou_none_p_kernel(tc, x_words, x_scales, w1, w2, gn, w3, res,
             nc.vector.tensor_tensor(wide[:, h, :], sm[:, h, :], ad[:, h, :], ALU.add)
             nc.vector.scalar_tensor_tensor(un[:, h, :], mx[:, h, :], 2.0, wide[:, h, :], ALU.mult, ALU.max)
             nc.vector.scalar_tensor_tensor(num[:, h, :], sm[:, h, :], 2.0, un[:, h, :], ALU.mult, ALU.subtract)
+            for t in range(h.start, h.stop):
+                nc.vector.tensor_scalar(gained[:, t, :], num[:, t, :], 0.0, gn_t[t][:], ALU.max, ALU.mult)
         for h in halves:
             nc.scalar.activation(rs[:, h, :], un[:, h, :], ACT.Abs_reciprocal_sqrt, bias=0.1)
+            nc.scalar.activation(rec[:, h, :], rs[:, h, :], ACT.Square)
 
-        w3_g = sb("w3_g", [P, N, PACK], BF16)
-        nc.scalar.copy(w3_g[:], w3_raw[:].rearrange("p j n -> p n j"))
-        w3_q = quant("w3q", w3_g[:].rearrange("p n j -> p (n j)"), N)
+        def cast_w3(copy, h, tag):
+            g = sb(f"w3g{h}", [P, N // 2, PACK], BF16, tag)
+            cols = slice(h * N // 2, (h + 1) * N // 2)
+            copy(g[:].rearrange("p (c i) j -> p c j i", i=4), w3_raw[:, :, cols].rearrange("p j (c i) -> p c j i", i=4))
+            return g
 
-        for h in halves:
-            nc.vector.scalar_tensor_tensor(q1[:, h, :], num[:, h, :], 0.0, rs[:, h, :], ALU.max, ALU.mult)
-        for t in range(PACK):
-            nc.vector.scalar_tensor_tensor(z[:, t, :], q1[:, t, :], gn_t[t][:], rs[:, t, :], ALU.mult, ALU.mult)
+        w3_g = [cast_w3(nc.vector.tensor_copy, 0, "mx"), cast_w3(nc.scalar.copy, 1, "un")]
+        w3_q = [quant("w3q0", w3_g[0][:].rearrange("p n j -> p (n j)"), N // 2)]
         z_g = sb("z_g", [P, V, PACK], BF16)
-        nc.vector.tensor_copy(z_g[:], z[:].rearrange("p t v -> p v t"))
+        nc.vector.tensor_tensor(
+            z_g[:].rearrange("p (c i) t -> p c t i", i=4),
+            gained[:].rearrange("p t (c i) -> p c t i", i=4),
+            rec[:].rearrange("p t (c i) -> p c t i", i=4),
+            ALU.mult,
+        )
         z_q = quant("zq", z_g[:].rearrange("p v t -> p (v t)"), V)
+        w3_q.append(quant("w3q1", w3_g[1][:].rearrange("p n j -> p (n j)"), N // 2))
 
-        for m in range(N // P):
-            bank = psum.tile([P, S], F32, name=f"obank{m}", tag=f"ybank{m}")
-            cols = slice(m * P, (m + 1) * P)
-            product(bank[:, :V], (w3_q[0][:, cols], w3_q[1][:, cols]), z_q[0][:], z_q[1][:])
-            o = sb(f"o{m}", [P, V], F32)
-            nc.vector.tensor_tensor(o[:], bank[:, :V], res_t[:, m, :], ALU.add)
-            nc.sync.dma_start(out[cols, :], o[:])
+        for h in range(2):
+            bank = psum.tile([P, 2, V], F32, name=f"obank{h}", tag=f"ybank{h}")
+            for e in range(2):
+                cols = slice(e * P, (e + 1) * P)
+                product(bank[:, e, :], (w3_q[h][0][:, cols], w3_q[h][1][:, cols]), z_q[0][:], z_q[1][:])
+            o = sb(f"o{h}", [P, 2, V], F32)
+            nc.vector.tensor_tensor(o[:], bank[:], res_t[:, 2 * h : 2 * h + 2, :], ALU.add)
+            nc.sync.dma_start(out[2 * h * P : (2 * h + 2) * P, :].rearrange("(e p) v -> p e v", p=P), o[:])

@@ -48,8 +48,8 @@ def tile_picked_boxiou_none_p_kernel(tc, x_words, x_scales, w1, w2, gn, w3, res,
         for q in range(4):
             nc.scalar.dma_start(xs[32 * q : 32 * q + 4, :].bitcast(I32), x_scales[0, 4 * q : 4 * q + 4, :].bitcast(I32))
         nc.scalar.activation(warm[:, 1:2], warm[:, 0:1], ACT.Sigmoid)
-        nc.sync.dma_start(two_t[:], two)
         nc.sync.dma_start(xw[:].bitcast(I32), x_words[0].rearrange("p c r -> p (c r)").bitcast(I32))
+        nc.sync.dma_start(two_t[:], two)
         nc.sync.dma_start(w2_raw[:], w2.rearrange("(p j) c -> p j c", j=PACK))
         nc.sync.dma_start(ba_t[:], ba)
         nc.sync.dma_start(bb_t[:], bb)
@@ -65,7 +65,6 @@ def tile_picked_boxiou_none_p_kernel(tc, x_words, x_scales, w1, w2, gn, w3, res,
         xa_s = sb("xa_s", [P, S], U8)
         xb_s = sb("xb_s", [P, S], U8)
         nc.vector.tensor_copy(xa_s[:], xs[:].indirect(offs_t[:]))
-        nc.vector.tensor_copy(xb_s[:], xs[:].indirect(two_t[:]))
 
         def cast_tile(copy, name, raw, t, tag=None):
             g = sb(name, [P, P * PACK], BF16, tag)
@@ -87,6 +86,7 @@ def tile_picked_boxiou_none_p_kernel(tc, x_words, x_scales, w1, w2, gn, w3, res,
         xa_w = sb("xa_w", [P, S], U32, "w1g2")
         xb_w = sb("xb_w", [P, S], U32)
         nc.vector.tensor_copy(xa_w[:], xw[:].indirect(offs_t[:]))
+        nc.vector.tensor_copy(xb_s[:], xs[:].indirect(two_t[:]))
         nc.vector.tensor_copy(xb_w[:], xw[:].indirect(two_t[:]))
 
         def middles(t):
@@ -105,14 +105,12 @@ def tile_picked_boxiou_none_p_kernel(tc, x_words, x_scales, w1, w2, gn, w3, res,
             for e in range(2):
                 nc.vector.tensor_tensor(dy[:, 2 * h + e, :], y_sb[2 * h + e][:].indirect(bb_t[:]), ya[:, e, :], ALU.subtract)
 
-        y_sb = [middles(0), middles(1)]
-        w2_g = [cast_tile(nc.vector.tensor_copy, f"w2g{t}", w2_raw, t, f"w1g{t}") for t in range(2)]
-        w2_q = [quant(f"w2q{t}", w2_g[t][:], P) for t in range(2)]
-        w2_g += [cast_tile(nc.scalar.copy, f"w2g{t}", w2_raw, t, f"w1q{t - 2}_c") for t in range(2, PACK)]
-        y_sb += [middles(2), middles(3)]
-        gaps(0, "w1g0")
-        w2_q += [quant(f"w2q{t}", w2_g[t][:], P) for t in range(2, PACK)]
-        gaps(1, "w1q1_c")
+        y_sb = [middles(t) for t in range(PACK)]
+        w2_q = []
+        for h in range(2):
+            w2_g = [cast_tile(nc.scalar.copy, "w2g3", w2_raw, t, "w1q3_c") if t == 3 else cast_tile(nc.vector.tensor_copy, f"w2g{t}", w2_raw, t) for t in (2 * h, 2 * h + 1)]
+            w2_q += [quant(f"w2q{2 * h + e}", w2_g[e][:], P) for e in range(2)]
+            gaps(h, ("w2g1", "w2g2")[h])
 
         ca = sb("ca", [P, PACK, V], F32)
         cb = sb("cb", [P, PACK, V], F32)
@@ -139,10 +137,14 @@ def tile_picked_boxiou_none_p_kernel(tc, x_words, x_scales, w1, w2, gn, w3, res,
         for h in halves:
             nc.vector.tensor_tensor(sm[:, h, :], ca[:, h, :], cb[:, h, :], ALU.add)
             nc.vector.tensor_tensor(mx[:, h, :], ca[:, h, :], cb[:, h, :], ALU.max)
-            nc.vector.tensor_tensor(wide[:, h, :], sm[:, h, :], ad[:, h, :], ALU.add)
-            nc.vector.scalar_tensor_tensor(un[:, h, :], mx[:, h, :], 2.0, wide[:, h, :], ALU.mult, ALU.max)
-            nc.vector.scalar_tensor_tensor(num[:, h, :], sm[:, h, :], 2.0, un[:, h, :], ALU.mult, ALU.subtract)
-            for t in range(h.start, h.stop):
+            pair = range(h.start, h.stop)
+            for t in pair:
+                nc.vector.tensor_tensor(wide[:, t, :], sm[:, t, :], ad[:, t, :], ALU.add)
+            for t in pair:
+                nc.vector.scalar_tensor_tensor(un[:, t, :], mx[:, t, :], 2.0, wide[:, t, :], ALU.mult, ALU.max)
+            for t in pair:
+                nc.vector.scalar_tensor_tensor(num[:, t, :], sm[:, t, :], 2.0, un[:, t, :], ALU.mult, ALU.subtract)
+            for t in pair:
                 nc.vector.tensor_scalar(gained[:, t, :], num[:, t, :], 0.0, gn_t[t][:], ALU.max, ALU.mult)
         for h in halves:
             nc.scalar.activation(rs[:, h, :], un[:, h, :], ACT.Abs_reciprocal_sqrt, bias=0.1)
@@ -166,11 +168,11 @@ def tile_picked_boxiou_none_p_kernel(tc, x_words, x_scales, w1, w2, gn, w3, res,
         z_q = quant("zq", z_g[:].rearrange("p v t -> p (v t)"), V)
         w3_q.append(quant("w3q1", w3_g[1][:].rearrange("p n j -> p (n j)"), N // 2))
 
-        for h in range(2):
-            bank = psum.tile([P, 2, V], F32, name=f"obank{h}", tag=f"ybank{h}")
-            for e in range(2):
-                cols = slice(e * P, (e + 1) * P)
-                product(bank[:, e, :], (w3_q[h][0][:, cols], w3_q[h][1][:, cols]), z_q[0][:], z_q[1][:])
-            o = sb(f"o{h}", [P, 2, V], F32)
-            nc.vector.tensor_tensor(o[:], bank[:], res_t[:, 2 * h : 2 * h + 2, :], ALU.add)
-            nc.sync.dma_start(out[2 * h * P : (2 * h + 2) * P, :].rearrange("(e p) v -> p e v", p=P), o[:])
+        for m in range(N // P):
+            h, e = divmod(m, 2)
+            bank = psum.tile([P, S], F32, name=f"obank{m}", tag=f"ybank{m}")
+            cols = slice(e * P, (e + 1) * P)
+            product(bank[:, :V], (w3_q[h][0][:, cols], w3_q[h][1][:, cols]), z_q[0][:], z_q[1][:])
+            o = sb(f"o{m}", [P, V], F32)
+            nc.vector.tensor_tensor(o[:], bank[:, :V], res_t[:, m, :], ALU.add)
+            (nc.sync, nc.scalar)[e].dma_start(out[m * P : (m + 1) * P, :], o[:])

@@ -33,6 +33,7 @@ def tile_picked_boxiou_none_p_kernel(tc, x_words, x_scales, w1, w2, gn, w3, res,
         bb_t = sb("bb_t", [P, V // 16], U16)
         xw = sb("xw", [P, T], U32)
         xs = sb("xs", [P, T], U8)
+        xs_in = sb("xs_in", [P, T], U8)
         w1_raw = sb("w1_raw", [P, PACK, H], F32)
         w2_raw = sb("w2_raw", [P, PACK, H], F32)
         w3_raw = sb("w3_raw", [P, PACK, N], F32)
@@ -44,12 +45,12 @@ def tile_picked_boxiou_none_p_kernel(tc, x_words, x_scales, w1, w2, gn, w3, res,
         nc.vector.memset(warm[:, 0:1], 0.0)
 
         nc.sync.dma_start(offs_t[:], offs)
-        nc.sync.dma_start(w1_raw[:], w1.rearrange("(p j) c -> p j c", j=PACK))
         for q in range(4):
-            nc.scalar.dma_start(xs[32 * q : 32 * q + 4, :].bitcast(I32), x_scales[0, 4 * q : 4 * q + 4, :].bitcast(I32))
+            (nc.scalar, nc.sync)[q // 2].dma_start(xs_in[32 * q : 32 * q + 4, :].bitcast(I32), x_scales[0, 4 * q : 4 * q + 4, :].bitcast(I32))
         nc.scalar.activation(warm[:, 1:2], warm[:, 0:1], ACT.Sigmoid)
-        nc.sync.dma_start(xw[:].bitcast(I32), x_words[0].rearrange("p c r -> p (c r)").bitcast(I32))
+        nc.sync.dma_start(w1_raw[:], w1.rearrange("(p j) c -> p j c", j=PACK))
         nc.sync.dma_start(two_t[:], two)
+        nc.sync.dma_start(xw[:].bitcast(I32), x_words[0].rearrange("p c r -> p (c r)").bitcast(I32))
         nc.sync.dma_start(w2_raw[:], w2.rearrange("(p j) c -> p j c", j=PACK))
         nc.sync.dma_start(ba_t[:], ba)
         nc.sync.dma_start(bb_t[:], bb)
@@ -64,7 +65,11 @@ def tile_picked_boxiou_none_p_kernel(tc, x_words, x_scales, w1, w2, gn, w3, res,
 
         xa_s = sb("xa_s", [P, S], U8)
         xb_s = sb("xb_s", [P, S], U8)
+        for q in range(4):
+            rows = slice(32 * q, 32 * q + 4)
+            nc.vector.tensor_copy(xs[rows, :].bitcast(I32), xs_in[rows, :].bitcast(I32))
         nc.vector.tensor_copy(xa_s[:], xs[:].indirect(offs_t[:]))
+        nc.vector.tensor_copy(xb_s[:], xs[:].indirect(two_t[:]))
 
         def cast_tile(copy, name, raw, t, tag=None):
             g = sb(name, [P, P * PACK], BF16, tag)
@@ -86,7 +91,6 @@ def tile_picked_boxiou_none_p_kernel(tc, x_words, x_scales, w1, w2, gn, w3, res,
         xa_w = sb("xa_w", [P, S], U32, "w1g2")
         xb_w = sb("xb_w", [P, S], U32)
         nc.vector.tensor_copy(xa_w[:], xw[:].indirect(offs_t[:]))
-        nc.vector.tensor_copy(xb_s[:], xs[:].indirect(two_t[:]))
         nc.vector.tensor_copy(xb_w[:], xw[:].indirect(two_t[:]))
 
         def middles(t):
@@ -108,9 +112,9 @@ def tile_picked_boxiou_none_p_kernel(tc, x_words, x_scales, w1, w2, gn, w3, res,
         y_sb = [middles(t) for t in range(PACK)]
         w2_q = []
         for h in range(2):
-            w2_g = [cast_tile(nc.scalar.copy, "w2g3", w2_raw, t, "w1q3_c") if t == 3 else cast_tile(nc.vector.tensor_copy, f"w2g{t}", w2_raw, t) for t in (2 * h, 2 * h + 1)]
+            w2_g = [cast_tile(nc.vector.tensor_copy, f"w2g{t}", w2_raw, t) for t in (2 * h, 2 * h + 1)]
             w2_q += [quant(f"w2q{2 * h + e}", w2_g[e][:], P) for e in range(2)]
-            gaps(h, ("w2g1", "w2g2")[h])
+            gaps(h, f"w2g{2 * h + 1}")
 
         ca = sb("ca", [P, PACK, V], F32)
         cb = sb("cb", [P, PACK, V], F32)

from contextlib import ExitStack

import concourse.mybir as mybir

K, T, S, V, N, H = 512, 2048, 512, 256, 512, 512
P = 128
PACK = 4
FLOPS = 2 * K * H * S * 2 + 2 * H * N * V

F32 = mybir.dt.float32
BF16 = mybir.dt.bfloat16
I32 = mybir.dt.int32
U32 = mybir.dt.uint32
U16 = mybir.dt.uint16
U8 = mybir.dt.uint8
FP8X4 = mybir.dt.float8_e4m3fn_x4
ALU = mybir.AluOpType
ACT = mybir.ActivationFunctionType


def tile_picked_boxiou_none_p_kernel(tc, x_words, x_scales, w1, w2, gn, w3, res, offs, two, ba, bb, out):
    nc = tc.nc
    with ExitStack() as ctx:
        keep = ctx.enter_context(tc.tile_pool(name="keep", bufs=1))
        psum = ctx.enter_context(tc.psum_pool(name="psum", bufs=1))

        def sb(name, shape, dtype, tag=None):
            return keep.tile(shape, dtype, name=name, tag=tag or name, align_bytes=64)

        offs_t = sb("offs_t", [P, S // 16], U16)
        two_t = sb("two_t", [P, S // 16], U16)
        ba_t = sb("ba_t", [P, V // 16], U16)
        bb_t = sb("bb_t", [P, V // 16], U16)
        xw = sb("xw", [P, T], U32)
        xs = sb("xs", [P, T], U8)
        xs_in = sb("xs_in", [P, T], U8)
        w1_raw = sb("w1_raw", [P, PACK, H], F32)
        w2_raw = sb("w2_raw", [P, PACK, H], F32)
        w3_raw = sb("w3_raw", [P, PACK, N], F32)
        res_t = sb("res_t", [P, N // P, V], F32)
        gn_t = [sb(f"gn{t}", [P, 1], F32) for t in range(PACK)]
        warm = sb("warm", [P, 2], F32)

        nc.vector.memset(xs[:].bitcast(I32), 0)
        nc.vector.memset(warm[:, 0:1], 0.0)

        nc.sync.dma_start(offs_t[:], offs)
        for q in range(4):
            (nc.scalar, nc.sync)[q // 2].dma_start(xs_in[32 * q : 32 * q + 4, :].bitcast(I32), x_scales[0, 4 * q : 4 * q + 4, :].bitcast(I32))
        nc.scalar.activation(warm[:, 1:2], warm[:, 0:1], ACT.Sigmoid)
        nc.sync.dma_start(w1_raw[:], w1.rearrange("(p j) c -> p j c", j=PACK))
        nc.sync.dma_start(two_t[:], two)
        nc.sync.dma_start(xw[:].bitcast(I32), x_words[0].rearrange("p c r -> p (c r)").bitcast(I32))
        nc.sync.dma_start(w2_raw[:], w2.rearrange("(p j) c -> p j c", j=PACK))
        nc.sync.dma_start(ba_t[:], ba)
        nc.sync.dma_start(bb_t[:], bb)
        w3_rows = w3.rearrange("(b j r) n -> j b r n", j=PACK, r=8)
        for j in range(PACK):
            nc.sync.dma_start(w3_raw[:, j, :], w3_rows[j])
        nc.sync.dma_start(res_t[:], res.rearrange("(t p) v -> p t v", p=P))
        gn_rows = gn.rearrange("(b j r) o -> j b r o", j=PACK, r=8)
        with nc.allow_non_contiguous_dma(reason="one gain for each feature"):
            for t in range(PACK):
                nc.sync.dma_start(gn_t[t][:], gn_rows[t])

        xa_s = sb("xa_s", [P, S], U8)
        xb_s = sb("xb_s", [P, S], U8)
        for q in range(4):
            rows = slice(32 * q, 32 * q + 4)
            nc.vector.tensor_copy(xs[rows, :].bitcast(I32), xs_in[rows, :].bitcast(I32))
        nc.vector.tensor_copy(xa_s[:], xs[:].indirect(offs_t[:]))
        nc.vector.tensor_copy(xb_s[:], xs[:].indirect(two_t[:]))

        def cast_tile(copy, name, raw, t, tag=None):
            g = sb(name, [P, P * PACK], BF16, tag)
            src = raw[:].rearrange("p j (b t h i) -> p t b h j i", t=PACK, h=2, i=4)[:, t]
            copy(g[:].rearrange("p (b h i j) -> p b h j i", h=2, i=4, j=PACK), src)
            return g

        def quant(name, g, cols):
            codes = sb(f"{name}_c", [P, cols], U32)
            scales = sb(f"{name}_s", [P, cols], U8)
            nc.vector.quantize_mx(out=codes[:].bitcast(FP8X4), scales=scales[:], in_=g)
            return codes, scales

        def product(bank, wq, xw_g, xs_g):
            nc.tensor.matmul_mx(out=bank, lhsT=wq[0].bitcast(FP8X4), lhsT_scale=wq[1], rhs=xw_g.bitcast(FP8X4), rhs_scale=xs_g, start=True, stop=True)

        w1_g = [cast_tile(nc.scalar.copy, f"w1g{t}", w1_raw, t) for t in range(PACK)]
        w1_q = [quant(f"w1q{t}", w1_g[t][:], P) for t in range(PACK)]
        xa_w = sb("xa_w", [P, S], U32, "w1g2")
        xb_w = sb("xb_w", [P, S], U32)
        nc.vector.tensor_copy(xa_w[:], xw[:].indirect(offs_t[:]))
        nc.vector.tensor_copy(xb_w[:], xw[:].indirect(two_t[:]))

        def middles(t):
            bank = psum.tile([P, S], F32, name=f"ybank{t}", tag=f"ybank{t}")
            product(bank[:], (w1_q[t][0][:], w1_q[t][1][:]), xa_w[:], xa_s[:])
            y = sb(f"y{t}", [P, S], F32)
            nc.scalar.copy(y[:], bank[:])
            return y

        dy = sb("dy", [P, PACK, V], F32)

        def gaps(h, tag):
            ya = sb(f"ya{h}", [P, 2, V], F32, tag)
            for e in range(2):
                nc.vector.tensor_copy(ya[:, e, :], y_sb[2 * h + e][:].indirect(ba_t[:]))
            for e in range(2):
                nc.vector.tensor_tensor(dy[:, 2 * h + e, :], y_sb[2 * h + e][:].indirect(bb_t[:]), ya[:, e, :], ALU.subtract)

        y_sb = [middles(t) for t in range(PACK)]
        w2_q = []
        for h in range(2):
            w2_g = [cast_tile(nc.vector.tensor_copy, f"w2g{t}", w2_raw, t) for t in (2 * h, 2 * h + 1)]
            w2_q += [quant(f"w2q{2 * h + e}", w2_g[e][:], P) for e in range(2)]
            gaps(h, f"w2g{2 * h + 1}")

        ca = sb("ca", [P, PACK, V], F32)
        cb = sb("cb", [P, PACK, V], F32)
        ad = sb("ad", [P, PACK, V], F32)
        for t in range(PACK):
            bank = psum.tile([P, S], F32, name=f"ubank{t}", tag=f"ubank{t}")
            product(bank[:], (w2_q[t][0][:], w2_q[t][1][:]), xb_w[:], xb_s[:])
            u = sb(f"u{t}", [P, S], F32)
            nc.scalar.copy(u[:], bank[:])
            nc.scalar.activation(ca[:, t, :], u[:].indirect(ba_t[:]), ACT.Sigmoid)
            nc.scalar.activation(cb[:, t, :], u[:].indirect(bb_t[:]), ACT.Sigmoid)
            if t % 2:
                nc.scalar.activation(ad[:, t - 1 : t + 1, :], dy[:, t - 1 : t + 1, :], ACT.Abs)

        sm = sb("sm", [P, PACK, V], F32)
        mx = sb("mx", [P, PACK, V], F32)
        wide = sb("wide", [P, PACK, V], F32)
        num = sb("num", [P, PACK, V], F32)
        un = sb("un", [P, PACK, V], F32)
        rs = sb("rs", [P, PACK, V], F32, "u3")
        rec = sb("rec", [P, PACK, V], F32)
        gained = sb("gained", [P, PACK, V], F32)
        halves = [slice(0, 2), slice(2, 4)]
        for h in halves:
            nc.vector.tensor_tensor(sm[:, h, :], ca[:, h, :], cb[:, h, :], ALU.add)
            nc.vector.tensor_tensor(mx[:, h, :], ca[:, h, :], cb[:, h, :], ALU.max)
            pair = range(h.start, h.stop)
            for t in pair:
                nc.vector.tensor_tensor(wide[:, t, :], sm[:, t, :], ad[:, t, :], ALU.add)
            for t in pair:
                nc.vector.scalar_tensor_tensor(un[:, t, :], mx[:, t, :], 2.0, wide[:, t, :], ALU.mult, ALU.max)
            for t in pair:
                nc.vector.scalar_tensor_tensor(num[:, t, :], sm[:, t, :], 2.0, un[:, t, :], ALU.mult, ALU.subtract)
            for t in pair:
                nc.vector.tensor_scalar(gained[:, t, :], num[:, t, :], 0.0, gn_t[t][:], ALU.max, ALU.mult)
        for h in halves:
            nc.scalar.activation(rs[:, h, :], un[:, h, :], ACT.Abs_reciprocal_sqrt, bias=0.1)
            nc.scalar.activation(rec[:, h, :], rs[:, h, :], ACT.Square)

        def cast_w3(copy, h, tag):
            g = sb(f"w3g{h}", [P, N // 2, PACK], BF16, tag)
            cols = slice(h * N // 2, (h + 1) * N // 2)
            copy(g[:].rearrange("p (c i) j -> p c j i", i=4), w3_raw[:, :, cols].rearrange("p j (c i) -> p c j i", i=4))
            return g

        w3_g = [cast_w3(nc.vector.tensor_copy, 0, "mx"), cast_w3(nc.scalar.copy, 1, "un")]
        w3_q = [quant("w3q0", w3_g[0][:].rearrange("p n j -> p (n j)"), N // 2)]
        z_g = sb("z_g", [P, V, PACK], BF16)
        nc.vector.tensor_tensor(
            z_g[:].rearrange("p (c i) t -> p c t i", i=4),
            gained[:].rearrange("p t (c i) -> p c t i", i=4),
            rec[:].rearrange("p t (c i) -> p c t i", i=4),
            ALU.mult,
        )
        z_q = quant("zq", z_g[:].rearrange("p v t -> p (v t)"), V)
        w3_q.append(quant("w3q1", w3_g[1][:].rearrange("p n j -> p (n j)"), N // 2))

        for m in range(N // P):
            h, e = divmod(m, 2)
            bank = psum.tile([P, S], F32, name=f"obank{m}", tag=f"ybank{m}")
            cols = slice(e * P, (e + 1) * P)
            product(bank[:, :V], (w3_q[h][0][:, cols], w3_q[h][1][:, cols]), z_q[0][:], z_q[1][:])
            o = sb(f"o{m}", [P, V], F32)
            nc.vector.tensor_tensor(o[:], bank[:, :V], res_t[:, m, :], ALU.add)
            (nc.sync, nc.scalar)[e].dma_start(out[m * P : (m + 1) * P, :], o[:])
